import numpy as np
import ml_dtypes


def mxq(x, axis, fmt="e4m3"):
    dtype, down = {"e4m3": (ml_dtypes.float8_e4m3fn, 7), "e5m2": (ml_dtypes.float8_e5m2, 14)}[fmt]
    v = np.moveaxis(np.asarray(x, np.float32).astype(ml_dtypes.bfloat16).astype(np.float64), axis, -1)
    blocks = v.reshape(v.shape[:-1] + (-1, 32))
    amax = np.abs(blocks).max(-1, keepdims=True)
    byte = np.maximum(np.where(amax > 0, np.frexp(amax)[1] - 1 + 127, 0) - down, 1)
    scale = np.exp2(byte - 127.0)
    codes = (blocks / scale).astype(np.float32).astype(dtype).astype(np.float64)
    return np.moveaxis((codes * scale).reshape(v.shape), -1, axis)


WIDE = False


def mx_kscale(k):
    if not WIDE:
        return np.ones(k)
    levels = np.array([10, -10, 5, -5, 0])
    if k % 512:
        return np.exp2(np.random.permutation(np.resize(levels, k // 32))).repeat(32)
    a = np.empty((k // 512, 16))
    for p in range(k // 512):
        a[p, :8] = np.random.permutation(np.resize(levels, 8))
        for g in range(8):
            far = levels[np.abs(levels - a[p, g]) >= 10]
            a[p, g + 8] = far[np.random.randint(len(far))]
    return np.exp2(a.ravel()).repeat(32)


def f64(x):
    return np.asarray(x).astype(np.float64)


def striped(idx):
    return np.tile(idx.reshape(-1, 16).T, (8, 1)).astype(np.uint16)


def unstriped(offs):
    return offs[:16].T.reshape(-1).astype(np.int64)


def pack_weight(w):
    k, n = w.shape
    w = f64(np.asarray(w, np.float32).astype(ml_dtypes.bfloat16)).reshape(k // 32, 32, n)
    amax = np.abs(w).max(1)
    byte = np.clip(np.where(amax > 0, np.frexp(amax)[1] - 1 + 127 - 7, 1), 1, 254)
    scaled = (w * np.exp2(127.0 - byte)[:, None, :]).reshape(k, n).astype(np.float32)
    words = np.ascontiguousarray(scaled.reshape(k // 512, 128, 4, n).transpose(0, 1, 3, 2)).astype(ml_dtypes.float8_e4m3fn).view(np.uint8)
    return words, np.ascontiguousarray(byte.astype(np.uint8).reshape(k // 512, 16, n))


def unpack_weight(words, scales):
    g, p, n, _ = words.shape
    vals = np.ascontiguousarray(words).view(ml_dtypes.float8_e4m3fn).astype(np.float64) * np.repeat(np.exp2(scales.astype(np.float64) - 127.0), 8, axis=1)[..., None]
    return vals.transpose(0, 1, 3, 2).reshape(g * 512, n)


K, T, S, N = 512, 2048, 512, 128


def setup_inputs():
    n = np.random.standard_normal
    s = mx_kscale(K)[:, None]
    packed_xT = pack_weight(n((K, T)) * s)
    return {
        "x_words": packed_xT[0],
        "x_scales": packed_xT[1],
        "w1": (n((K, N)) / np.sqrt(K) / s).astype(np.float32),
        "guide": (n((N, S))).astype(np.float32),
        "reg": (np.random.uniform(0.1, 0.6, (N, 1))).astype(np.float32),
        "offs": striped(np.random.permutation(T)[:S]),
        "wa": striped(np.random.permutation(S)),
        "wb": striped(np.random.permutation(S)),
        "wc": striped(np.random.permutation(S)),
    }


def reference(x_words, x_scales, w1, guide, reg, offs, wa, wb, wc):
    xq = unpack_weight(x_words, x_scales)[:, unstriped(offs)]
    y = mxq(f64(w1), 0, "e4m3").T @ xq
    gy = f64(guide) * y
    mgy = (gy + gy[:, unstriped(wa)] + gy[:, unstriped(wb)]) / 3
    mg = (f64(guide) + f64(guide)[:, unstriped(wa)] + f64(guide)[:, unstriped(wb)]) / 3
    my = (y + y[:, unstriped(wa)] + y[:, unstriped(wb)]) / 3
    mgg = ((f64(guide)) ** 2 + (f64(guide)[:, unstriped(wa)]) ** 2 + (f64(guide)[:, unstriped(wb)]) ** 2) / 3
    sl = (mgy - (mg * my)) / (mgg - ((mg) ** 2) + f64(reg))
    ic = my - (sl * mg)
    base = (0.5 * (sl[:, unstriped(wb)] + sl[:, unstriped(wc)])) * f64(guide) + 0.5 * (ic[:, unstriped(wb)] + ic[:, unstriped(wc)])
    return y + 1.5 * (y - base)

@@ -1,0 +1,178 @@
+import math
+from contextlib import ExitStack
+
+import concourse.mybir as mybir
+
+K, T, S, N = 512, 2048, 512, 128
+FLOPS = 2 * K * N * S
+
+F32 = mybir.dt.float32
+BF16 = mybir.dt.bfloat16
+I32 = mybir.dt.int32
+U32 = mybir.dt.uint32
+U16 = mybir.dt.uint16
+U8 = mybir.dt.uint8
+FP8X4 = mybir.dt.float8_e4m3fn_x4
+ACT = mybir.ActivationFunctionType
+ADD = mybir.AluOpType.add
+SUB = mybir.AluOpType.subtract
+MUL = mybir.AluOpType.mult
+
+P = 128
+PACK = 4
+HALF = S // 2
+PER_COL = 16
+
+
+def tile_picked_yguid_det_p_kernel(tc, x_words, x_scales, w1, guide, reg, offs, wa, wb, wc, out):
+    nc = tc.nc
+    with ExitStack() as ctx:
+        lists = ctx.enter_context(tc.tile_pool(name="lists", bufs=1))
+        sb = ctx.enter_context(tc.tile_pool(name="sb", bufs=1))
+        psum = ctx.enter_context(tc.psum_pool(name="psum", bufs=1))
+
+        def row(name):
+            return sb.tile([P, S], F32, name=name, align_bytes=64)
+
+        halves = [slice(h * HALF, (h + 1) * HALF) for h in range(2)]
+
+        def part(lst, h):
+            return lst[:, h * HALF // PER_COL : (h + 1) * HALF // PER_COL]
+
+        def fetch(dst, window, lst, h):
+            nc.scalar.activation(out=dst[:, halves[h]], in_=window[:].indirect(part(lst, h)), func=ACT.Copy)
+
+        def tt(dst, a, b, op):
+            nc.vector.tensor_tensor(out=dst, in0=a, in1=b, op=op)
+
+        def stt(dst, a, c, b, op1):
+            nc.vector.scalar_tensor_tensor(out=dst, in0=a, scalar=c, in1=b, op0=MUL, op1=op1)
+
+        offs_t = lists.tile([P, S // PER_COL], U16, name="offs_t")
+        wa_t = lists.tile([P, S // PER_COL], U16, name="wa_t")
+        wb_t = lists.tile([P, S // PER_COL], U16, name="wb_t")
+        wc_t = lists.tile([P, S // PER_COL], U16, name="wc_t")
+
+        xs = sb.tile([P, T], U8, name="xs", tag="small", align_bytes=64)
+        xw = sb.tile([P, T], U32, name="xw", tag="big", align_bytes=64)
+        g0 = row("g0")
+        reg_t = sb.tile([P, 1], F32, name="reg_t")
+        w_raw = sb.tile([P, PACK, N], F32, name="w_raw", align_bytes=64)
+
+        nc.vector.memset(xs[:].bitcast(I32), 0)
+        warm = sb.tile([P, 1], F32, name="warm")
+        warm2 = sb.tile([P, 1], F32, name="warm2")
+        nc.gpsimd.memset(warm[:], 1.0)
+        nc.scalar.activation(out=warm2[:], in_=warm[:], func=ACT.Abs_reciprocal_sqrt)
+        nc.sync.dma_start(offs_t[:], offs)
+        nc.sync.dma_start(wa_t[:], wa)
+        nc.sync.dma_start(out=g0[:], in_=guide)
+        for q in range(4):
+            nc.sync.dma_start(out=xs[32 * q : 32 * q + 4, :].bitcast(I32), in_=x_scales[0, 4 * q : 4 * q + 4, :].bitcast(I32))
+        nc.sync.dma_start(out=xw[:].bitcast(I32), in_=x_words[0].rearrange("p n t -> p (n t)").bitcast(I32))
+        nc.sync.dma_start(wb_t[:], wb)
+        nc.sync.dma_start(wc_t[:], wc)
+        nc.gpsimd.dma_start(out=w_raw[:], in_=w1.rearrange("(p j) m -> p j m", j=PACK))
+        nc.gpsimd.dma_start(out=reg_t[:], in_=reg)
+
+        ps = sb.tile([P, S], U8, name="ps", align_bytes=64)
+        pw = sb.tile([P, S], U32, name="pw", align_bytes=64)
+        nc.vector.tensor_copy(out=ps[:], in_=xs[:].indirect(offs_t[:]))
+
+        w_bf = sb.tile([P, N, PACK], BF16, name="w_bf", tag="small", align_bytes=64)
+        w_codes = sb.tile([P, N], U32, name="w_codes", align_bytes=64)
+        w_scales = sb.tile([P, N], U8, name="w_scales", align_bytes=64)
+        nc.gpsimd.tensor_copy(out=w_bf[:], in_=w_raw[:].rearrange("p j m -> p m j"))
+        nc.vector.quantize_mx(out=w_codes[:].bitcast(FP8X4), scales=w_scales[:], in_=w_bf[:].rearrange("p m j -> p (m j)"))
+
+        g1, g2 = row("g1"), row("g2")
+        gm2, gp2, den, rs, inv = row("gm2"), row("gp2"), row("den"), row("rs"), row("inv")
+        for h in range(2):
+            fetch(g1, g0, wa_t, h)
+        for h in range(2):
+            fetch(g2, g0, wb_t, h)
+
+        def contrasts(h, gq, gm, gp):
+            c = halves[h]
+            tt(gq, g1[:, c], g2[:, c], ADD)
+            tt(gm, g1[:, c], g2[:, c], SUB)
+            stt(gp, g0[:, c], -2.0, gq, ADD)
+
+        def squares(h, gm, gp):
+            c = halves[h]
+            nc.scalar.activation(out=gm2[:, c], in_=gm, func=ACT.Square, scale=math.sqrt(3.0))
+            nc.scalar.activation(out=gp2[:, c], in_=gp, func=ACT.Square)
+
+        early = sb.tile([P, 3, HALF], F32, name="early", align_bytes=64)
+        contrasts(0, early[:, 0, :], early[:, 1, :], early[:, 2, :])
+        squares(0, early[:, 1, :], early[:, 2, :])
+
+        y0 = row("y0")
+        banks = [psum.tile([P, HALF], F32, name=f"bank{h}") for h in range(2)]
+        for h in range(2):
+            c = halves[h]
+            nc.vector.tensor_copy(out=pw[:, c], in_=xw[:].indirect(part(offs_t, h)))
+            nc.tensor.matmul_mx(out=banks[h][:], lhsT=w_codes[:].bitcast(FP8X4), lhsT_scale=w_scales[:],
+                                rhs=pw[:, c].bitcast(FP8X4), rhs_scale=ps[:, c], start=True, stop=True)
+            nc.scalar.copy(out=y0[:, c], in_=banks[h][:])
+
+        late = sb.tile([P, 5, HALF], F32, name="late", tag="big", align_bytes=64)
+        contrasts(1, late[:, 0, :], late[:, 1, :], late[:, 2, :])
+        gq = [early[:, 0, :], late[:, 0, :]]
+        gm = [early[:, 1, :], late[:, 1, :]]
+        gp = [early[:, 2, :], late[:, 2, :]]
+        gs = [late[:, 3, :], late[:, 4, :]]
+        for h in range(2):
+            tt(gs[h], gq[h], g0[:, halves[h]], ADD)
+
+        y1, y2, yq, ym, yp, ys = row("y1"), row("y2"), row("yq"), row("ym"), row("yp"), row("ys")
+        t1, t2, num, sl, u, ic = row("t1"), row("t2"), row("num"), row("sl"), row("u"), row("ic")
+        fetch(y2, y0, wb_t, 0)
+        fetch(y2, y0, wb_t, 1)
+        fetch(y1, y0, wa_t, 1)
+        squares(1, gm[1], gp[1])
+        tt(den[:], gm2[:], gp2[:], ADD)
+        nc.scalar.activation(out=rs[:], in_=den[:], func=ACT.Abs_reciprocal_sqrt, scale=1.0 / 18.0, bias=reg_t[:])
+        nc.scalar.activation(out=inv[:], in_=rs[:], func=ACT.Square)
+        for h in range(2):
+            c = halves[h]
+            if h == 0:
+                tt(yq[:, c], y0[:].indirect(part(wa_t, h)), y2[:, c], ADD)
+            else:
+                tt(yq[:, c], y1[:, c], y2[:, c], ADD)
+            stt(ym[:, c], y2[:, c], -2.0, yq[:, c], ADD)
+            stt(yp[:, c], banks[h][:], -2.0, yq[:, c], ADD)
+            tt(t2[:, c], gm[h], ym[:, c], MUL)
+            tt(t1[:, c], gp[h], yp[:, c], MUL)
+        for h in range(2):
+            c = halves[h]
+            stt(num[:, c], t2[:, c], 3.0, t1[:, c], ADD)
+        for h in range(2):
+            c = halves[h]
+            stt(sl[:, c], num[:, c], -0.75 / 18.0, inv[:, c], MUL)
+
+        s1, s2, i2 = row("s1"), row("s2"), row("i2")
+        for h in range(2):
+            fetch(s1, sl, wb_t, h)
+            fetch(s2, sl, wc_t, h)
+        for h in range(2):
+            c = halves[h]
+            tt(ys[:, c], banks[h][:], yq[:, c], ADD)
+            stt(u[:, c], sl[:, c], 1.0 / 3.0, gs[h], MUL)
+        for h in range(2):
+            c = halves[h]
+            stt(ic[:, c], ys[:, c], -0.25, u[:, c], SUB)
+        for h in range(2):
+            fetch(i2, ic, wc_t, h)
+
+        ss, sg, o1, o2, o3 = row("ss"), row("sg"), row("o1"), row("o2"), row("o3")
+        for h in range(2):
+            c = halves[h]
+            tt(ss[:, c], s1[:, c], s2[:, c], ADD)
+            tt(sg[:, c], ss[:, c], g0[:, c], MUL)
+            stt(o1[:, c], banks[h][:], 2.5, sg[:, c], ADD)
+        for h in range(2):
+            c = halves[h]
+            tt(o2[:, c], ic[:].indirect(part(wb_t, h)), o1[:, c], ADD)
+            tt(o3[:, c], o2[:, c], i2[:, c], ADD)
+            nc.sync.dma_start(out=out[:, c], in_=o3[:, c])

@@ -2,6 +2,7 @@ import math
 from contextlib import ExitStack
 
 import concourse.mybir as mybir
+from concourse.masks import make_identity
 
 K, T, S, N = 512, 2048, 512, 128
 FLOPS = 2 * K * N * S
@@ -31,8 +32,8 @@ def tile_picked_yguid_det_p_kernel(tc, x_words, x_scales, w1, guide, reg, offs, 
         sb = ctx.enter_context(tc.tile_pool(name="sb", bufs=1))
         psum = ctx.enter_context(tc.psum_pool(name="psum", bufs=1))
 
-        def row(name):
-            return sb.tile([P, S], F32, name=name, align_bytes=64)
+        def row(name, tag=None):
+            return sb.tile([P, S], F32, name=name, tag=tag or name, align_bytes=64)
 
         halves = [slice(h * HALF, (h + 1) * HALF) for h in range(2)]
 
@@ -53,59 +54,65 @@ def tile_picked_yguid_det_p_kernel(tc, x_words, x_scales, w1, guide, reg, offs, 
         wb_t = lists.tile([P, S // PER_COL], U16, name="wb_t")
         wc_t = lists.tile([P, S // PER_COL], U16, name="wc_t")
 
-        xs = sb.tile([P, T], U8, name="xs", tag="small", align_bytes=64)
+        xs = sb.tile([P, T], U8, name="xs", tag="xs", align_bytes=64)
         xw = sb.tile([P, T], U32, name="xw", tag="big", align_bytes=64)
         g0 = row("g0")
         reg_t = sb.tile([P, 1], F32, name="reg_t")
+        ident = sb.tile([P, P], F32, name="ident", tag="ident", align_bytes=64)
+        make_identity(nc, ident[:])
         w_raw = sb.tile([P, PACK, N], F32, name="w_raw", align_bytes=64)
 
         nc.vector.memset(xs[:].bitcast(I32), 0)
         warm = sb.tile([P, 1], F32, name="warm")
         warm2 = sb.tile([P, 1], F32, name="warm2")
-        nc.gpsimd.memset(warm[:], 1.0)
+        nc.vector.memset(warm[:], 1.0)
         nc.scalar.activation(out=warm2[:], in_=warm[:], func=ACT.Abs_reciprocal_sqrt)
         nc.sync.dma_start(offs_t[:], offs)
         nc.sync.dma_start(wa_t[:], wa)
         nc.sync.dma_start(out=g0[:], in_=guide)
+        nc.sync.dma_start(wb_t[:], wb)
+        nc.sync.dma_start(out=w_raw[:], in_=w1.rearrange("(p j) m -> p j m", j=PACK))
         for q in range(4):
             nc.sync.dma_start(out=xs[32 * q : 32 * q + 4, :].bitcast(I32), in_=x_scales[0, 4 * q : 4 * q + 4, :].bitcast(I32))
         nc.sync.dma_start(out=xw[:].bitcast(I32), in_=x_words[0].rearrange("p n t -> p (n t)").bitcast(I32))
-        nc.sync.dma_start(wb_t[:], wb)
         nc.sync.dma_start(wc_t[:], wc)
-        nc.gpsimd.dma_start(out=w_raw[:], in_=w1.rearrange("(p j) m -> p j m", j=PACK))
-        nc.gpsimd.dma_start(out=reg_t[:], in_=reg)
+        nc.sync.dma_start(out=reg_t[:], in_=reg)
+
+        def turned_sum(bank, block, terms):
+            for i, term in enumerate(terms):
+                nc.tensor.matmul(bank[:, block * P : (block + 1) * P], lhsT=term, rhs=ident[:], is_transpose=True,
+                                 start=(i == 0), stop=(i == len(terms) - 1))
+
+        def blk(tile, block):
+            return tile[:, block * P : (block + 1) * P]
 
         ps = sb.tile([P, S], U8, name="ps", align_bytes=64)
-        pw = sb.tile([P, S], U32, name="pw", align_bytes=64)
-        nc.vector.tensor_copy(out=ps[:], in_=xs[:].indirect(offs_t[:]))
+        pw = sb.tile([P, S], U32, name="pw", tag="pw", align_bytes=64)
 
-        w_bf = sb.tile([P, N, PACK], BF16, name="w_bf", tag="small", align_bytes=64)
+        w_bf = sb.tile([P, N, PACK], BF16, name="w_bf", align_bytes=64)
         w_codes = sb.tile([P, N], U32, name="w_codes", align_bytes=64)
         w_scales = sb.tile([P, N], U8, name="w_scales", align_bytes=64)
-        nc.gpsimd.tensor_copy(out=w_bf[:], in_=w_raw[:].rearrange("p j m -> p m j"))
+        nc.vector.tensor_copy(out=w_bf[:], in_=w_raw[:].rearrange("p j m -> p m j"))
         nc.vector.quantize_mx(out=w_codes[:].bitcast(FP8X4), scales=w_scales[:], in_=w_bf[:].rearrange("p m j -> p (m j)"))
+        nc.vector.tensor_copy(out=ps[:], in_=xs[:].indirect(offs_t[:]))
 
         g1, g2 = row("g1"), row("g2")
-        gm2, gp2, den, rs, inv = row("gm2"), row("gp2"), row("den"), row("rs"), row("inv")
+        rs, inv, gs_s = row("rs"), row("inv"), row("gs_s")
+        gs_t = [psum.tile([P, HALF], F32, name=f"gs_t{h}", tag=f"stage{h}") for h in range(2)]
+        gs = psum.tile([P, S], F32, name="gs")
         for h in range(2):
             fetch(g1, g0, wa_t, h)
-        for h in range(2):
             fetch(g2, g0, wb_t, h)
+        for h in range(2):
+            for b in range(2):
+                turned_sum(gs_t[h], b, [blk(g0, 2 * h + b), blk(g1, 2 * h + b), blk(g2, 2 * h + b)])
+            nc.scalar.copy(out=gs_s[:, halves[h]], in_=gs_t[h][:])
+        for b in range(4):
+            turned_sum(gs, b, [blk(gs_s, b)])
 
-        def contrasts(h, gq, gm, gp):
-            c = halves[h]
-            tt(gq, g1[:, c], g2[:, c], ADD)
-            tt(gm, g1[:, c], g2[:, c], SUB)
-            stt(gp, g0[:, c], -2.0, gq, ADD)
-
-        def squares(h, gm, gp):
-            c = halves[h]
-            nc.scalar.activation(out=gm2[:, c], in_=gm, func=ACT.Square, scale=math.sqrt(3.0))
-            nc.scalar.activation(out=gp2[:, c], in_=gp, func=ACT.Square)
-
-        early = sb.tile([P, 3, HALF], F32, name="early", align_bytes=64)
-        contrasts(0, early[:, 0, :], early[:, 1, :], early[:, 2, :])
-        squares(0, early[:, 1, :], early[:, 2, :])
+        gm, gm2 = row("gm", "xs"), row("gm2", "gs_s")
+        tt(gm[:], g1[:], g2[:], SUB)
+        nc.scalar.activation(out=gm2[:], in_=gm[:], func=ACT.Square, scale=math.sqrt(3.0 / 18.0))
 
         y0 = row("y0")
         banks = [psum.tile([P, HALF], F32, name=f"bank{h}") for h in range(2)]
@@ -116,34 +123,36 @@ def tile_picked_yguid_det_p_kernel(tc, x_words, x_scales, w1, guide, reg, offs, 
                                 rhs=pw[:, c].bitcast(FP8X4), rhs_scale=ps[:, c], start=True, stop=True)
             nc.scalar.copy(out=y0[:, c], in_=banks[h][:])
 
-        late = sb.tile([P, 5, HALF], F32, name="late", tag="big", align_bytes=64)
-        contrasts(1, late[:, 0, :], late[:, 1, :], late[:, 2, :])
-        gq = [early[:, 0, :], late[:, 0, :]]
-        gm = [early[:, 1, :], late[:, 1, :]]
-        gp = [early[:, 2, :], late[:, 2, :]]
-        gs = [late[:, 3, :], late[:, 4, :]]
-        for h in range(2):
-            tt(gs[h], gq[h], g0[:, halves[h]], ADD)
+        gp = sb.tile([P, S], F32, name="gp", tag="big", align_bytes=64)
+        stt(gp[:], g0[:], -3.0, gs[:], ADD)
+        gp2 = row("gp2", "pw")
 
-        y1, y2, yq, ym, yp, ys = row("y1"), row("y2"), row("yq"), row("ym"), row("yp"), row("ys")
+        y1, y2, yq, ym, yp = row("y1"), row("y2"), row("yq"), row("ym"), row("yp")
         t1, t2, num, sl, u, ic = row("t1"), row("t2"), row("num"), row("sl"), row("u"), row("ic")
+        nc.vector.tensor_copy(out=y1[:, halves[0]], in_=y0[:].indirect(part(wa_t, 0)))
         fetch(y2, y0, wb_t, 0)
+        nc.scalar.activation(out=gp2[:], in_=gp[:], func=ACT.Square, scale=math.sqrt(1.0 / 18.0))
         fetch(y2, y0, wb_t, 1)
         fetch(y1, y0, wa_t, 1)
-        squares(1, gm[1], gp[1])
-        tt(den[:], gm2[:], gp2[:], ADD)
-        nc.scalar.activation(out=rs[:], in_=den[:], func=ACT.Abs_reciprocal_sqrt, scale=1.0 / 18.0, bias=reg_t[:])
+        den = row("den")
+        tt(den[:], gp2[:], gm2[:], ADD)
+        nc.scalar.activation(out=rs[:], in_=den[:], func=ACT.Abs_reciprocal_sqrt, bias=reg_t[:])
         nc.scalar.activation(out=inv[:], in_=rs[:], func=ACT.Square)
         for h in range(2):
             c = halves[h]
-            if h == 0:
-                tt(yq[:, c], y0[:].indirect(part(wa_t, h)), y2[:, c], ADD)
-            else:
-                tt(yq[:, c], y1[:, c], y2[:, c], ADD)
-            stt(ym[:, c], y2[:, c], -2.0, yq[:, c], ADD)
+            tt(yq[:, c], y1[:, c], y2[:, c], ADD)
+            tt(ym[:, c], y1[:, c], y2[:, c], SUB)
             stt(yp[:, c], banks[h][:], -2.0, yq[:, c], ADD)
-            tt(t2[:, c], gm[h], ym[:, c], MUL)
-            tt(t1[:, c], gp[h], yp[:, c], MUL)
+            tt(t2[:, c], gm[:, c], ym[:, c], MUL)
+            tt(t1[:, c], gp[:, c], yp[:, c], MUL)
+        ys_t = psum.tile([P, S], F32, name="ys_t", tag="stage1")
+        ys = psum.tile([P, S], F32, name="ys")
+        ys_s = row("ys_s")
+        for b in range(4):
+            turned_sum(ys_t, b, [blk(y0, b), blk(yq, b)])
+        nc.scalar.copy(out=ys_s[:], in_=ys_t[:])
+        for b in range(4):
+            turned_sum(ys, b, [blk(ys_s, b)])
         for h in range(2):
             c = halves[h]
             stt(num[:, c], t2[:, c], 3.0, t1[:, c], ADD)
@@ -151,28 +160,33 @@ def tile_picked_yguid_det_p_kernel(tc, x_words, x_scales, w1, guide, reg, offs, 
             c = halves[h]
             stt(sl[:, c], num[:, c], -0.75 / 18.0, inv[:, c], MUL)
 
-        s1, s2, i2 = row("s1"), row("s2"), row("i2")
+        s1, s2, i1, i2 = row("s1", "yq"), row("s2"), row("i1"), row("i2")
         for h in range(2):
             fetch(s1, sl, wb_t, h)
             fetch(s2, sl, wc_t, h)
         for h in range(2):
             c = halves[h]
-            tt(ys[:, c], banks[h][:], yq[:, c], ADD)
-            stt(u[:, c], sl[:, c], 1.0 / 3.0, gs[h], MUL)
+            stt(u[:, c], sl[:, c], 1.0 / 3.0, gs[:, c], MUL)
         for h in range(2):
             c = halves[h]
             stt(ic[:, c], ys[:, c], -0.25, u[:, c], SUB)
         for h in range(2):
             fetch(i2, ic, wc_t, h)
+        fetch(i1, ic, wb_t, 1)
 
-        ss, sg, o1, o2, o3 = row("ss"), row("sg"), row("o1"), row("o2"), row("o3")
-        for h in range(2):
-            c = halves[h]
-            tt(ss[:, c], s1[:, c], s2[:, c], ADD)
-            tt(sg[:, c], ss[:, c], g0[:, c], MUL)
-            stt(o1[:, c], banks[h][:], 2.5, sg[:, c], ADD)
-        for h in range(2):
-            c = halves[h]
-            tt(o2[:, c], ic[:].indirect(part(wb_t, h)), o1[:, c], ADD)
-            tt(o3[:, c], o2[:, c], i2[:, c], ADD)
-            nc.sync.dma_start(out=out[:, c], in_=o3[:, c])
+        a, b = halves
+        y25 = row("y25", "rs")
+        ss, sg, o1, o2, o3 = row("ss", "u"), row("sg"), row("o1"), row("o2"), row("o3")
+        nc.scalar.mul(out=y25[:, a], in_=banks[0][:], mul=2.5)
+        tt(ss[:, a], s1[:, a], s2[:, a], ADD)
+        tt(o1[:, a], ic[:].indirect(part(wb_t, 0)), y25[:, a], ADD)
+        tt(sg[:, a], ss[:, a], g0[:, a], MUL)
+        tt(o2[:, a], sg[:, a], o1[:, a], ADD)
+        tt(ss[:, b], s1[:, b], s2[:, b], ADD)
+        tt(o3[:, a], o2[:, a], i2[:, a], ADD)
+        nc.sync.dma_start(out=out[:, a], in_=o3[:, a])
+        tt(sg[:, b], ss[:, b], g0[:, b], MUL)
+        stt(o1[:, b], banks[1][:], 2.5, i2[:, b], ADD)
+        tt(o2[:, b], sg[:, b], o1[:, b], ADD)
+        tt(o3[:, b], o2[:, b], i1[:, b], ADD)
+        nc.sync.dma_start(out=out[:, b], in_=o3[:, b])

@@ -89,6 +89,9 @@ def tile_picked_yguid_det_p_kernel(tc, x_words, x_scales, w1, guide, reg, offs, 
         ps = sb.tile([P, S], U8, name="ps", align_bytes=64)
         pw = sb.tile([P, S], U32, name="pw", tag="pw", align_bytes=64)
 
+        g1, g2 = row("g1"), row("g2")
+        nc.vector.tensor_copy(out=g1[:, halves[0]], in_=g0[:].indirect(part(wa_t, 0)))
+
         w_bf = sb.tile([P, N, PACK], BF16, name="w_bf", align_bytes=64)
         w_codes = sb.tile([P, N], U32, name="w_codes", align_bytes=64)
         w_scales = sb.tile([P, N], U8, name="w_scales", align_bytes=64)
@@ -96,13 +99,12 @@ def tile_picked_yguid_det_p_kernel(tc, x_words, x_scales, w1, guide, reg, offs, 
         nc.vector.quantize_mx(out=w_codes[:].bitcast(FP8X4), scales=w_scales[:], in_=w_bf[:].rearrange("p m j -> p (m j)"))
         nc.vector.tensor_copy(out=ps[:], in_=xs[:].indirect(offs_t[:]))
 
-        g1, g2 = row("g1"), row("g2")
         rs, inv, gs_s = row("rs"), row("inv"), row("gs_s")
         gs_t = [psum.tile([P, HALF], F32, name=f"gs_t{h}", tag=f"stage{h}") for h in range(2)]
         gs = psum.tile([P, S], F32, name="gs")
-        for h in range(2):
-            fetch(g1, g0, wa_t, h)
-            fetch(g2, g0, wb_t, h)
+        fetch(g2, g0, wb_t, 0)
+        fetch(g1, g0, wa_t, 1)
+        fetch(g2, g0, wb_t, 1)
         for h in range(2):
             for b in range(2):
                 turned_sum(gs_t[h], b, [blk(g0, 2 * h + b), blk(g1, 2 * h + b), blk(g2, 2 * h + b)])

import math
from contextlib import ExitStack

import concourse.mybir as mybir
from concourse.masks import make_identity

K, T, S, N = 512, 2048, 512, 128
FLOPS = 2 * K * N * S

F32 = mybir.dt.float32
BF16 = mybir.dt.bfloat16
I32 = mybir.dt.int32
U32 = mybir.dt.uint32
U16 = mybir.dt.uint16
U8 = mybir.dt.uint8
FP8X4 = mybir.dt.float8_e4m3fn_x4
ACT = mybir.ActivationFunctionType
ADD = mybir.AluOpType.add
SUB = mybir.AluOpType.subtract
MUL = mybir.AluOpType.mult

P = 128
PACK = 4
HALF = S // 2
PER_COL = 16


def tile_picked_yguid_det_p_kernel(tc, x_words, x_scales, w1, guide, reg, offs, wa, wb, wc, out):
    nc = tc.nc
    with ExitStack() as ctx:
        lists = ctx.enter_context(tc.tile_pool(name="lists", bufs=1))
        sb = ctx.enter_context(tc.tile_pool(name="sb", bufs=1))
        psum = ctx.enter_context(tc.psum_pool(name="psum", bufs=1))

        def row(name, tag=None):
            return sb.tile([P, S], F32, name=name, tag=tag or name, align_bytes=64)

        halves = [slice(h * HALF, (h + 1) * HALF) for h in range(2)]

        def part(lst, h):
            return lst[:, h * HALF // PER_COL : (h + 1) * HALF // PER_COL]

        def fetch(dst, window, lst, h):
            nc.scalar.activation(out=dst[:, halves[h]], in_=window[:].indirect(part(lst, h)), func=ACT.Copy)

        def tt(dst, a, b, op):
            nc.vector.tensor_tensor(out=dst, in0=a, in1=b, op=op)

        def stt(dst, a, c, b, op1):
            nc.vector.scalar_tensor_tensor(out=dst, in0=a, scalar=c, in1=b, op0=MUL, op1=op1)

        offs_t = lists.tile([P, S // PER_COL], U16, name="offs_t")
        wa_t = lists.tile([P, S // PER_COL], U16, name="wa_t")
        wb_t = lists.tile([P, S // PER_COL], U16, name="wb_t")
        wc_t = lists.tile([P, S // PER_COL], U16, name="wc_t")

        xs = sb.tile([P, T], U8, name="xs", tag="xs", align_bytes=64)
        xw = sb.tile([P, T], U32, name="xw", tag="big", align_bytes=64)
        g0 = row("g0")
        reg_t = sb.tile([P, 1], F32, name="reg_t")
        ident = sb.tile([P, P], F32, name="ident", tag="ident", align_bytes=64)
        make_identity(nc, ident[:])
        w_raw = sb.tile([P, PACK, N], F32, name="w_raw", align_bytes=64)

        nc.vector.memset(xs[:].bitcast(I32), 0)
        warm = sb.tile([P, 1], F32, name="warm")
        warm2 = sb.tile([P, 1], F32, name="warm2")
        nc.vector.memset(warm[:], 1.0)
        nc.scalar.activation(out=warm2[:], in_=warm[:], func=ACT.Abs_reciprocal_sqrt)
        nc.sync.dma_start(offs_t[:], offs)
        nc.sync.dma_start(wa_t[:], wa)
        nc.sync.dma_start(out=g0[:], in_=guide)
        nc.sync.dma_start(wb_t[:], wb)
        nc.sync.dma_start(out=w_raw[:], in_=w1.rearrange("(p j) m -> p j m", j=PACK))
        for q in range(4):
            nc.sync.dma_start(out=xs[32 * q : 32 * q + 4, :].bitcast(I32), in_=x_scales[0, 4 * q : 4 * q + 4, :].bitcast(I32))
        nc.sync.dma_start(out=xw[:].bitcast(I32), in_=x_words[0].rearrange("p n t -> p (n t)").bitcast(I32))
        nc.sync.dma_start(wc_t[:], wc)
        nc.sync.dma_start(out=reg_t[:], in_=reg)

        def turned_sum(bank, block, terms):
            for i, term in enumerate(terms):
                nc.tensor.matmul(bank[:, block * P : (block + 1) * P], lhsT=term, rhs=ident[:], is_transpose=True,
                                 start=(i == 0), stop=(i == len(terms) - 1))

        def blk(tile, block):
            return tile[:, block * P : (block + 1) * P]

        ps = sb.tile([P, S], U8, name="ps", align_bytes=64)
        pw = sb.tile([P, S], U32, name="pw", tag="pw", align_bytes=64)

        g1, g2 = row("g1"), row("g2")
        nc.vector.tensor_copy(out=g1[:, halves[0]], in_=g0[:].indirect(part(wa_t, 0)))

        w_bf = sb.tile([P, N, PACK], BF16, name="w_bf", align_bytes=64)
        w_codes = sb.tile([P, N], U32, name="w_codes", align_bytes=64)
        w_scales = sb.tile([P, N], U8, name="w_scales", align_bytes=64)
        nc.vector.tensor_copy(out=w_bf[:], in_=w_raw[:].rearrange("p j m -> p m j"))
        nc.vector.quantize_mx(out=w_codes[:].bitcast(FP8X4), scales=w_scales[:], in_=w_bf[:].rearrange("p m j -> p (m j)"))
        nc.vector.tensor_copy(out=ps[:], in_=xs[:].indirect(offs_t[:]))

        rs, inv, gs_s = row("rs"), row("inv"), row("gs_s")
        gs_t = [psum.tile([P, HALF], F32, name=f"gs_t{h}", tag=f"stage{h}") for h in range(2)]
        gs = psum.tile([P, S], F32, name="gs")
        fetch(g2, g0, wb_t, 0)
        fetch(g1, g0, wa_t, 1)
        fetch(g2, g0, wb_t, 1)
        for h in range(2):
            for b in range(2):
                turned_sum(gs_t[h], b, [blk(g0, 2 * h + b), blk(g1, 2 * h + b), blk(g2, 2 * h + b)])
            nc.scalar.copy(out=gs_s[:, halves[h]], in_=gs_t[h][:])
        for b in range(4):
            turned_sum(gs, b, [blk(gs_s, b)])

        gm, gm2 = row("gm", "xs"), row("gm2", "gs_s")
        tt(gm[:], g1[:], g2[:], SUB)
        nc.scalar.activation(out=gm2[:], in_=gm[:], func=ACT.Square, scale=math.sqrt(3.0 / 18.0))

        y0 = row("y0")
        banks = [psum.tile([P, HALF], F32, name=f"bank{h}") for h in range(2)]
        for h in range(2):
            c = halves[h]
            nc.vector.tensor_copy(out=pw[:, c], in_=xw[:].indirect(part(offs_t, h)))
            nc.tensor.matmul_mx(out=banks[h][:], lhsT=w_codes[:].bitcast(FP8X4), lhsT_scale=w_scales[:],
                                rhs=pw[:, c].bitcast(FP8X4), rhs_scale=ps[:, c], start=True, stop=True)
            nc.scalar.copy(out=y0[:, c], in_=banks[h][:])

        gp = sb.tile([P, S], F32, name="gp", tag="big", align_bytes=64)
        stt(gp[:], g0[:], -3.0, gs[:], ADD)
        gp2 = row("gp2", "pw")

        y1, y2, yq, ym, yp = row("y1"), row("y2"), row("yq"), row("ym"), row("yp")
        t1, t2, num, sl, u, ic = row("t1"), row("t2"), row("num"), row("sl"), row("u"), row("ic")
        nc.vector.tensor_copy(out=y1[:, halves[0]], in_=y0[:].indirect(part(wa_t, 0)))
        fetch(y2, y0, wb_t, 0)
        nc.scalar.activation(out=gp2[:], in_=gp[:], func=ACT.Square, scale=math.sqrt(1.0 / 18.0))
        fetch(y2, y0, wb_t, 1)
        fetch(y1, y0, wa_t, 1)
        den = row("den")
        tt(den[:], gp2[:], gm2[:], ADD)
        nc.scalar.activation(out=rs[:], in_=den[:], func=ACT.Abs_reciprocal_sqrt, bias=reg_t[:])
        nc.scalar.activation(out=inv[:], in_=rs[:], func=ACT.Square)
        for h in range(2):
            c = halves[h]
            tt(yq[:, c], y1[:, c], y2[:, c], ADD)
            tt(ym[:, c], y1[:, c], y2[:, c], SUB)
            stt(yp[:, c], banks[h][:], -2.0, yq[:, c], ADD)
            tt(t2[:, c], gm[:, c], ym[:, c], MUL)
            tt(t1[:, c], gp[:, c], yp[:, c], MUL)
        ys_t = psum.tile([P, S], F32, name="ys_t", tag="stage1")
        ys = psum.tile([P, S], F32, name="ys")
        ys_s = row("ys_s")
        for b in range(4):
            turned_sum(ys_t, b, [blk(y0, b), blk(yq, b)])
        nc.scalar.copy(out=ys_s[:], in_=ys_t[:])
        for b in range(4):
            turned_sum(ys, b, [blk(ys_s, b)])
        for h in range(2):
            c = halves[h]
            stt(num[:, c], t2[:, c], 3.0, t1[:, c], ADD)
        for h in range(2):
            c = halves[h]
            stt(sl[:, c], num[:, c], -0.75 / 18.0, inv[:, c], MUL)

        s1, s2, i1, i2 = row("s1", "yq"), row("s2"), row("i1"), row("i2")
        for h in range(2):
            fetch(s1, sl, wb_t, h)
            fetch(s2, sl, wc_t, h)
        for h in range(2):
            c = halves[h]
            stt(u[:, c], sl[:, c], 1.0 / 3.0, gs[:, c], MUL)
        for h in range(2):
            c = halves[h]
            stt(ic[:, c], ys[:, c], -0.25, u[:, c], SUB)
        for h in range(2):
            fetch(i2, ic, wc_t, h)
        fetch(i1, ic, wb_t, 1)

        a, b = halves
        y25 = row("y25", "rs")
        ss, sg, o1, o2, o3 = row("ss", "u"), row("sg"), row("o1"), row("o2"), row("o3")
        nc.scalar.mul(out=y25[:, a], in_=banks[0][:], mul=2.5)
        tt(ss[:, a], s1[:, a], s2[:, a], ADD)
        tt(o1[:, a], ic[:].indirect(part(wb_t, 0)), y25[:, a], ADD)
        tt(sg[:, a], ss[:, a], g0[:, a], MUL)
        tt(o2[:, a], sg[:, a], o1[:, a], ADD)
        tt(ss[:, b], s1[:, b], s2[:, b], ADD)
        tt(o3[:, a], o2[:, a], i2[:, a], ADD)
        nc.sync.dma_start(out=out[:, a], in_=o3[:, a])
        tt(sg[:, b], ss[:, b], g0[:, b], MUL)
        stt(o1[:, b], banks[1][:], 2.5, i2[:, b], ADD)
        tt(o2[:, b], sg[:, b], o1[:, b], ADD)
        tt(o3[:, b], o2[:, b], i1[:, b], ADD)
        nc.sync.dma_start(out=out[:, b], in_=o3[:, b])
